import numpy as np, ml_dtypes
CORES = [16,32,48,64,80]
N = 5
import mx_ref
NC, NZ = 128, 256
BF = ml_dtypes.bfloat16
def setup_inputs(rng):
    def f(*shape):
        return mx_ref.flush((rng.standard_normal(shape, dtype=np.float32) * np.exp2(rng.integers(-2, 3, shape[:-1] + (1,)))).astype(BF))
    return {"w": f(N, 128, 512), "x": f(N, 128, 4 * NC), "d": f(N, 128, N * 512), "z": f(N, 128, 4 * NZ)}
def setup_inputs_blocks(rng):
    d = setup_inputs(rng)
    for k in ("w", "x", "d", "z"): d[k] = mx_ref.spread(d[k], rng, 2)
    return d
def setup_inputs_wide(rng):
    d = setup_inputs(rng)
    for k in ("w", "x", "d", "z"): d[k] = mx_ref.flush((d[k].astype(np.float32) * np.exp2(rng.integers(-8, 9, (N, 1, 1))).astype(np.float32)).astype(BF))
    return d
def setup_inputs_zeros(rng):
    d = setup_inputs(rng); v = d["x"].reshape(N, 128, -1, 4).copy()
    v[np.broadcast_to((rng.random((N, 1, v.shape[2], 1)) < 0.33), v.shape)] = 0
    d["x"] = v.reshape(d["x"].shape)
    return d
def reference(w, x, d, z):
    QX = [mx_ref.quantize(x[j]) for j in range(N)]; QZ = [mx_ref.quantize(z[j]) for j in range(N)]
    y = np.zeros((N, 128, N * NC), np.float32); h = np.zeros((N, 128, NZ), np.float32)
    for r in range(N):
        qw = mx_ref.quantize(w[r])
        for j in range(N):
            y[r][:, NC * j:NC * j + NC] = mx_ref.matmul(qw, QX[j])
            p = mx_ref.matmul(mx_ref.quantize(d[r][:, 512 * j:512 * j + 512]), QZ[j])
            h[r] = p if j == 0 else h[r] + p
    return {"y": y, "h": h}

from concourse.bass import DstId, RemoteDMATransfer
from concourse.mybir import dt, ActivationFunctionType

N = 5
XW, ZW = 128, 256
NEAR, FAR = "near", "far"

CALLS = (
    (("xs", (NEAR, 0), (1, 2), (0, 8)), ("xs", (FAR, 0), (3, 4), (8, 8))),
    (("xc", (NEAR, 1), (1, 2), (0, 8)), ("xc", (FAR, 1), (3, 4), (8, 8))),
    (("zc", (NEAR, 2), (1, 2), (0, 8)), ("zc", (FAR, 2), (3, 4), (8, 8))),
    (("zs", (NEAR, 0), (1, 2), (0, 8)), ("zs", (FAR, 0), (3, 4), (8, 8))),
)
ARRIVE = (1, 3, 2, 4)
GATED = True

SCRATCH = {
    "xb": ("sbuf", [128, 4 * XW], "bfloat16"),
    "zb": ("sbuf", [128, 4 * ZW], "bfloat16"),
    "wb": ("sbuf", [128, 512], "bfloat16"),
    "db": ("sbuf", [128, N * 512], "bfloat16"),
    "xq": ("sbuf", [128, N * XW], "float8_e4m3fn_x4"),
    "xs": ("sbuf", [128, N * XW], "uint8"),
    "zq": ("sbuf", [128, N * ZW], "float8_e4m3fn_x4"),
    "zs": ("sbuf", [128, N * ZW], "uint8"),
    "wq": ("sbuf", [128, 128], "float8_e4m3fn_x4"),
    "ws": ("sbuf", [128, 128], "uint8"),
    "dq": ("sbuf", [128, N * 128], "float8_e4m3fn_x4"),
    "ds": ("sbuf", [128, N * 128], "uint8"),
    "yo": ("sbuf", [128, N * 128], "float32"),
    "ho": ("sbuf", [128, ZW], "float32"),
    "py": ("psum", [128, N * 512], "float32"),
    "ph": ("psum", [128, 512], "float32"),
}
SEMAPHORES = (["lx", "lz", "lw", "ld", "qx", "qz", "qw", "sent", "mh", "ch", "sy", "sh", "in0", "in1", "in2"]
              + ["%s%d" % (p, j) for p in ("qd", "ax", "az", "my", "cy") for j in range(N)])


def piece(T, name, r):
    if name == "xc":
        return T.xq[:, XW * r:XW * (r + 1)].bitcast(dt.uint8)
    if name == "xs":
        return T.xs[:, XW * r:XW * (r + 1)]
    if name == "zs":
        return T.zs[:, ZW * r:ZW * (r + 1)]
    a, b = {"zc": (0, ZW), "zl": (0, ZW // 2), "zh": (ZW // 2, ZW)}[name]
    return T.zq[:, ZW * r + a:ZW * r + b].bitcast(dt.uint8)


def engines(mask):
    return [i for i in range(mask.bit_length()) if (mask >> i) & 1]


def submask(mask, first, count):
    return sum(1 << i for i in engines(mask)[first:first + count])


def helpers(R, T, topo):
    mine = [c for c in range(topo.CHIPS * topo.CORES_PER_CHIP)
            if topo.chip(c) == topo.chip(R) and c != R and all(topo.may_write(c, d) for d in T.cores if d != R)]
    return {NEAR: [c for c in mine if topo.die(c) == topo.die(R)],
            FAR: [c for c in mine if topo.die(c) != topo.die(R)]}


def transfer(T, topo, name, r, dsts, mask, sem):
    ap = piece(T, name, r)
    ids = [DstId(rid=topo.addr(d)[0], pnc=topo.addr(d)[1]) for d in dsts]
    return RemoteDMATransfer(dst_ids=ids, dma_engine_mask=mask, remote_sem=sem, srcs=[ap], dsts=[ap for _ in dsts])


def last_hop_engines(T, topo, leg, r):
    name, via, offs, (first, count) = leg
    if via is None:
        return count
    R = T.cores[r]
    h = helpers(R, T, topo)[via[0]][via[1]]
    return len(engines(topo.mask(h, T.cores[(r + offs[0]) % N])))


def expected(T, topo, fam, j, r):
    off = (r - j) % N
    return sum(last_hop_engines(T, topo, leg, j) for call in CALLS for leg in call if leg[0][0] == fam and off in leg[2])


def arrive_sem(T, name, r):
    return T.sem["a%s%d" % (name[0], r)]


def helper_program(g, core, T, topo, r):
    R = T.cores[r]
    hs = helpers(R, T, topo)
    left, k = 0, 0
    for call in CALLS:
        for name, via, offs, (first, count) in call:
            if via is None or hs[via[0]][via[1]] != core:
                continue
            dsts = [T.cores[(r + o) % N] for o in offs]
            mask = topo.mask(core, dsts[0])
            g.wait_ge(T.sem["in%d" % k], count)
            g.remote_dma_fused([transfer(T, topo, name, r, dsts, mask, arrive_sem(T, name, r))], local_sem=T.sem.sent)
            left += len(engines(mask))
            k += 1
    if left:
        g.wait_ge(T.sem.sent, left)


def rank_core(g, core, T, topo, r):
    S = T.sem
    hs = helpers(core, T, topo)
    xcol = slice(XW * r, XW * (r + 1))
    zcol = slice(ZW * r, ZW * (r + 1))
    order = [r] + [(r - o) % N for o in ARRIVE]

    g.sync.dma_start(T.xb[:], T.x[:]).then_inc(S.lx, 16)
    g.sync.dma_start(T.zb[:], T.z[:]).then_inc(S.lz, 16)

    v = g.vector
    v.wait_ge(S.lx, 16)
    v.quantize_mx(T.xq[:, xcol], T.xs[:, xcol], T.xb[:]).then_inc(S.qx, 1)
    v.wait_ge(S.lz, 16)
    v.quantize_mx(T.zq[:, zcol], T.zs[:, zcol], T.zb[:]).then_inc(S.qz, 1)

    sent, seen, tasks = 0, set(), {}
    for call in CALLS:
        trs = []
        for name, via, offs, (first, count) in call:
            if name[0] not in seen:
                seen.add(name[0])
                g.wait_ge(S["q" + name[0]], 1)
            if via is None:
                dsts = [T.cores[(r + o) % N] for o in offs]
                sem = arrive_sem(T, name, r)
            else:
                h = hs[via[0]][via[1]]
                dsts = [h]
                sem = S["in%d" % tasks.get(h, 0)]
                tasks[h] = tasks.get(h, 0) + 1
            trs.append(transfer(T, topo, name, r, dsts, submask(topo.mask(core, dsts[0]), first, count), sem))
            sent += count
        g.remote_dma_fused(trs, local_sem=S.sent)

    (g.sync if GATED else g).wait_ge(S.sent, sent)
    g.sync.dma_start(T.wb[:], T.w[:]).then_inc(S.lw, 16)
    g.sync.dma_start(T.db[:], T.d[:]).then_inc(S.ld, 16)
    v.wait_ge(S.lw, 16)
    v.quantize_mx(T.wq[:], T.ws[:], T.wb[:]).then_inc(S.qw, 1)
    v.wait_ge(S.ld, 16)
    for j in order:
        v.quantize_mx(T.dq[:, 128 * j:128 * (j + 1)], T.ds[:, 128 * j:128 * (j + 1)],
                      T.db[:, 512 * j:512 * (j + 1)]).then_inc(S["qd%d" % j], 1)

    t = g.tensor
    t.wait_ge(S.qw, 1)
    for k, j in enumerate(order):
        if j == r:
            t.wait_ge(S.qx, 1)
        else:
            t.wait_ge(S["ax%d" % j], expected(T, topo, "x", j, r))
        t.matmul_mx(T.py[:, 512 * j:512 * j + XW], T.wq[:], T.ws[:], T.xq[:, XW * j:XW * (j + 1)],
                    T.xs[:, XW * j:XW * (j + 1)], True, True).then_inc(S["my%d" % j], 1)
        if j == r:
            t.wait_ge(S.qz, 1)
        else:
            t.wait_ge(S["az%d" % j], expected(T, topo, "z", j, r))
        t.wait_ge(S["qd%d" % j], 1)
        mm = t.matmul_mx(T.ph[:, 0:ZW], T.dq[:, 128 * j:128 * (j + 1)], T.ds[:, 128 * j:128 * (j + 1)],
                         T.zq[:, ZW * j:ZW * (j + 1)], T.zs[:, ZW * j:ZW * (j + 1)], k == 0, k == N - 1)
    mm.then_inc(S.mh, 1)

    s = g.scalar
    for j in order:
        blk = slice(128 * j, 128 * (j + 1))
        s.wait_ge(S["my%d" % j], 1)
        s.activation(T.yo[:, blk], T.py[:, 512 * j:512 * j + XW], ActivationFunctionType.Copy).then_inc(S["cy%d" % j], 1)
        s.wait_ge(S["cy%d" % j], 1)
        s.dma_start(T.y[:, blk], T.yo[:, blk]).then_inc(S.sy, 16)
    s.wait_ge(S.sy, 16 * N)

    v.wait_ge(S.mh, 1)
    v.tensor_copy(T.ho[:], T.ph[:, 0:ZW]).then_inc(S.ch, 1)
    g.sync.wait_ge(S.ch, 1)
    g.sync.dma_start(T.h[:], T.ho[:]).then_inc(S.sh, 16)
    g.sync.wait_ge(S.sh, 16)


def rank_program(g, core, T, topo):
    r = T.rank_of(core)
    if r is not None:
        rank_core(g, core, T, topo, r)
        return
    for q, R in enumerate(T.cores):
        if topo.chip(R) == topo.chip(core):
            helper_program(g, core, T, topo, q)
